import numpy as np
import ml_dtypes


def mxq(x, axis, fmt="e4m3"):
    dtype, down = {"e4m3": (ml_dtypes.float8_e4m3fn, 7), "e5m2": (ml_dtypes.float8_e5m2, 14)}[fmt]
    v = np.moveaxis(np.asarray(x, np.float32).astype(ml_dtypes.bfloat16).astype(np.float64), axis, -1)
    blocks = v.reshape(v.shape[:-1] + (-1, 32))
    amax = np.abs(blocks).max(-1, keepdims=True)
    byte = np.maximum(np.where(amax > 0, np.frexp(amax)[1] - 1 + 127, 0) - down, 1)
    scale = np.exp2(byte - 127.0)
    codes = (blocks / scale).astype(np.float32).astype(dtype).astype(np.float64)
    return np.moveaxis((codes * scale).reshape(v.shape), -1, axis)


WIDE = False


def mx_kscale(k):
    if not WIDE:
        return np.ones(k)
    levels = np.array([10, -10, 5, -5, 0])
    if k % 512:
        return np.exp2(np.random.permutation(np.resize(levels, k // 32))).repeat(32)
    a = np.empty((k // 512, 16))
    for p in range(k // 512):
        a[p, :8] = np.random.permutation(np.resize(levels, 8))
        for g in range(8):
            far = levels[np.abs(levels - a[p, g]) >= 10]
            a[p, g + 8] = far[np.random.randint(len(far))]
    return np.exp2(a.ravel()).repeat(32)


BF16 = ml_dtypes.bfloat16


def bf(x):
    return np.asarray(x, np.float32).astype(BF16)


def f64(x):
    return np.asarray(x).astype(np.float64)


E2M1 = np.array([0.0, 0.5, 1.0, 1.5, 2.0, 3.0, 4.0, 6.0, -0.0, -0.5, -1.0, -1.5, -2.0, -3.0, -4.0, -6.0])


def pack_weight(w, fmt):
    k, n = w.shape
    w = f64(bf(w)).reshape(k // 32, 32, n)
    amax = np.abs(w).max(1)
    if fmt == "e4m3":
        byte = np.frexp(amax)[1] - 1 + 127 - 7
    else:
        mant, ex = np.frexp(amax / 6.0)
        byte = np.where(mant > 0.5, ex, ex - 1) + 127
    byte = np.clip(np.where(amax > 0, byte, 1), 1, 254)
    scaled = (w * np.exp2(127.0 - byte)[:, None, :]).reshape(k, n).astype(np.float32)
    by_word = np.ascontiguousarray(scaled.reshape(k // 512, 128, 4, n).transpose(0, 1, 3, 2))
    if fmt == "e4m3":
        words = by_word.astype(ml_dtypes.float8_e4m3fn).view(np.uint8)
    else:
        c = by_word.astype(ml_dtypes.float4_e2m1fn).view(np.uint8) & 0xF
        words = c[..., 0::2] | (c[..., 1::2] << 4)
    return np.ascontiguousarray(words), np.ascontiguousarray(byte.astype(np.uint8).reshape(k // 512, 16, n))


def unpack_weight(words, scales, fmt):
    g, p, n, _ = words.shape
    if fmt == "e4m3":
        vals = np.ascontiguousarray(words).view(ml_dtypes.float8_e4m3fn).astype(np.float64)
    else:
        nib = np.empty((g, p, n, 4), np.uint8)
        nib[..., 0::2] = words & 0xF
        nib[..., 1::2] = words >> 4
        vals = E2M1[nib]
    vals = vals * np.repeat(np.exp2(scales.astype(np.float64) - 127.0), 8, axis=1)[..., None]
    return vals.transpose(0, 1, 3, 2).reshape(g * 512, n)
def pack4(w):
    words, scales = pack_weight(w, "e2m1")
    return words.reshape(words.shape[0], 128, -1), scales


def unpack4(words, scales):
    return unpack_weight(words.reshape(words.shape[0], 128, -1, 2), scales, "e2m1")


M, K, N = 1024, 2048, 512

SHARP = 2.0
GAIN = 3.0


def setup_inputs():
    s = mx_kscale(K)
    log_kernel = bf(-SHARP * np.square(np.random.standard_normal((M, K))))
    amplitude = bf((1 + 0.1 * np.random.standard_normal(K)) * s)
    w_static = GAIN * np.random.standard_normal((K, N)) / np.sqrt(K) / s[:, None]
    w_moving = GAIN * np.random.standard_normal((K, N)) / np.sqrt(K) / s[:, None]
    w_gate = GAIN * np.random.standard_normal((K, N)) / np.sqrt(K) / s[:, None]
    static_words, static_scales = pack4(w_static)
    moving_words, moving_scales = pack_weight(w_moving, "e4m3")
    return {"log_kernel": log_kernel, "amplitude": amplitude,
            "static_words": static_words, "static_scales": static_scales,
            "moving_words": moving_words, "moving_scales": moving_scales,
            "w_gate": bf(w_gate)}


def reference(log_kernel, amplitude, static_words, static_scales, moving_words, moving_scales, w_gate):
    phi = np.exp(f64(log_kernel)) * f64(amplitude)
    phi_q = mxq(phi, 1, "e4m3")
    static = phi_q @ unpack4(static_words, static_scales)
    moving = phi_q @ unpack_weight(moving_words, moving_scales, "e4m3")
    gate = phi_q @ mxq(f64(w_gate), 0, "e4m3")
    trust = 1 / (1 + np.exp(-gate))
    logit = static + trust * moving
    return 1 / (1 + np.exp(-logit))

@@ -1,0 +1,340 @@
+from contextlib import ExitStack
+
+import concourse.mybir as mybir
+from concourse.masks import make_identity
+
+ROWS, K, N = 1024, 2048, 512
+FLOPS = 3 * 2 * ROWS * K * N
+
+F32 = mybir.dt.float32
+BF16 = mybir.dt.bfloat16
+U32 = mybir.dt.uint32
+I32 = mybir.dt.int32
+U8 = mybir.dt.uint8
+E4M3X4 = mybir.dt.float8_e4m3fn_x4
+E2M1X4 = mybir.dt.float4_e2m1fn_x4
+ACT = mybir.ActivationFunctionType
+ALU = mybir.AluOpType
+
+P = 128
+PACK = 4
+K_PASS = P * PACK
+PASSES = K // K_PASS
+TILES = ROWS // P
+HALF = PASSES // 2
+LAST_EXP_STEP = TILES - 3
+
+
+def tile_hilbert_occupancy_map_s10_kernel(
+    tc, log_kernel, amplitude, static_words, static_scales, moving_words, moving_scales, w_gate, out
+):
+    nc = tc.nc
+    with ExitStack() as ctx:
+        keep = ctx.enter_context(tc.tile_pool(name="keep", bufs=1))
+        stage = ctx.enter_context(tc.tile_pool(name="stage", bufs=4))
+        psum = ctx.enter_context(tc.psum_pool(name="psum", bufs=1))
+        ctx.enter_context(tc.manual_schedule())
+
+        identity = keep.tile([P, P], F32, name="identity")
+        make_identity(nc, identity[:])
+        st_scales = keep.tile([P, PASSES, N], U8, name="st_scales", align_bytes=64)
+        mv_scales = keep.tile([P, PASSES, N], U8, name="mv_scales", align_bytes=64)
+        warm = keep.tile([P, 1], F32, name="warm")
+        nc.vector.memset(warm[:], 0.0)
+        nc.vector.memset(st_scales[:].rearrange("p g n -> p (g n)").bitcast(I32), 0)
+        nc.vector.memset(mv_scales[:].rearrange("p g n -> p (g n)").bitcast(I32), 0)
+        warm_out = keep.tile([P, 1], F32, name="warm_out")
+
+        amp = keep.tile([P, PASSES, 1, PACK], BF16, name="amp")
+        nc.scalar.dma_start(out=amp[:, :, 0, :], in_=amplitude.rearrange("(g p t) -> p g t", g=PASSES, t=PACK))
+
+        nc.scalar.activation(warm_out[:], warm[:], ACT.Exp)
+
+        x_tiles = []
+        for m in range(TILES):
+            x_tiles.append(keep.tile([P, K], BF16, name=f"x{m}", align_bytes=64))
+
+        def load_x(m, parts):
+            width = K // parts
+            for i in range(parts):
+                cols = slice(i * width, (i + 1) * width)
+                nc.sync.dma_start(out=x_tiles[m][:, cols], in_=log_kernel[m * P : (m + 1) * P, cols])
+
+        def load_scales(plane, source):
+            for q in range(4):
+                nc.sync.dma_start(
+                    out=plane[32 * q : 32 * q + 4, :, :].bitcast(I32),
+                    in_=source[:, 4 * q : 4 * q + 4, :].rearrange("g r n -> r g n").bitcast(I32),
+                )
+
+        st_words = keep.tile([P, PASSES, 2 * N], U8, name="st_words", align_bytes=64)
+        mv_words = keep.tile([P, PASSES, 4 * N], U8, name="mv_words", align_bytes=64)
+        raw = []
+        for g in range(PASSES):
+            raw.append(keep.tile([P, PACK, N], BF16, name=f"raw{g}", align_bytes=64))
+
+        def load_gate(g):
+            nc.sync.dma_start(
+                out=raw[g][:], in_=w_gate[g * K_PASS : (g + 1) * K_PASS, :].rearrange("(p j) n -> p j n", j=PACK)
+            )
+
+        def load_moving(g0, n):
+            nc.sync.dma_start(
+                out=mv_words[:, g0 : g0 + n, :], in_=moving_words[g0 : g0 + n].rearrange("g p n t -> p g (n t)")
+            )
+
+        load_x(0, 2)
+        load_scales(st_scales, static_scales)
+        load_x(1, 1)
+        nc.sync.dma_start(out=st_words[:], in_=static_words.rearrange("g p b -> p g b"))
+        load_gate(0)
+        load_gate(1)
+        load_gate(2)
+        load_x(2, 1)
+        load_scales(mv_scales, moving_scales)
+        load_moving(0, 2)
+        load_gate(3)
+        load_moving(2, 2)
+        for m in range(3, TILES):
+            load_x(m, 1)
+
+        phi_codes = keep.tile([P, TILES, PASSES, P], U32, name="phi_codes", align_bytes=64)
+        phi_scales = keep.tile([P, TILES, PASSES, P], U8, name="phi_scales", align_bytes=64)
+        gate_codes = keep.tile([P, PASSES, N], U32, name="gate_codes", align_bytes=64)
+        gate_scales = keep.tile([P, PASSES, N], U8, name="gate_scales", align_bytes=64)
+
+        exp_tiles = {}
+        phi_tiles = {}
+        turned = {}
+        gate_tiles = {}
+
+        def turn(m, h):
+            bank = psum.tile([P, 2 * HALF, P], F32, name=f"turn_{m}_{h}", tag=f"turn{h}")
+            turned[m, h] = bank
+            words = x_tiles[m][:].bitcast(F32)
+            for i in range(HALF):
+                first = (HALF * h + i) * (K_PASS // 2)
+                for u in range(2):
+                    nc.tensor.transpose(bank[:, 2 * i + u, :], words[:, first + u : first + K_PASS // 2 : 2], identity[:])
+
+        def exps(m, h):
+            tile = stage.tile([P, HALF, P, PACK], F32, name=f"exp_{m}_{h}", tag="exp", bufs=12)
+            exp_tiles[m, h] = tile
+            bank = turned[m, h][:].rearrange("p b r -> p (b r)").bitcast(BF16)
+            for i in range(HALF):
+                src = bank[:, 512 * i : 512 * (i + 1)].rearrange("p (u r e) -> p r u e", u=2, e=2)
+                nc.scalar.activation(tile[:, i, :, :].rearrange("p r (u e) -> p r u e", u=2), src, ACT.Exp)
+
+        def amplify(m, h, i0, n):
+            if (m, h) not in phi_tiles:
+                phi_tiles[m, h] = stage.tile([P, HALF, P, PACK], BF16, name=f"phi_{m}_{h}", tag="phi", bufs=4, align_bytes=64)
+            g = HALF * h + i0
+            nc.vector.tensor_tensor(
+                out=phi_tiles[m, h][:, i0 : i0 + n, :, :],
+                in0=exp_tiles[m, h][:, i0 : i0 + n, :, :],
+                in1=amp[:, g : g + n, :, :].to_broadcast([P, n, P, PACK]),
+                op=ALU.mult,
+            )
+
+        def quantize(m, h, i0, n):
+            g = HALF * h + i0
+            nc.vector.quantize_mx(
+                out=phi_codes[:, m, g : g + n, :].rearrange("p g r -> p (g r)").bitcast(E4M3X4),
+                scales=phi_scales[:, m, g : g + n, :].rearrange("p g r -> p (g r)"),
+                in_=phi_tiles[m, h][:, i0 : i0 + n, :, :].rearrange("p g r t -> p (g r t)"),
+            )
+
+        def gather_gate(g, copy, cols=slice(0, N)):
+            if g not in gate_tiles:
+                gate_tiles[g] = stage.tile([P, N, PACK], BF16, name=f"gate_{g}", tag="gate", bufs=4, align_bytes=64)
+            copy(out=gate_tiles[g][:, cols, :], in_=raw[g][:, :, cols].rearrange("p j n -> p n j"))
+
+        def quantize_gate(g):
+            nc.vector.quantize_mx(
+                out=gate_codes[:, g, :].bitcast(E4M3X4),
+                scales=gate_scales[:, g, :],
+                in_=gate_tiles[g][:].rearrange("p n t -> p (n t)"),
+            )
+
+        banks = {}
+
+        def bank_of(kind, m):
+            if (kind, m) not in banks:
+                banks[kind, m] = psum.tile([P, N], F32, name=f"{kind}_{m}", tag=f"{kind}{m % 2}")
+            return banks[kind, m]
+
+        def weight(kind, g, cols):
+            if kind == "static":
+                return st_words[:, g, 2 * cols.start : 2 * cols.stop].bitcast(E2M1X4), st_scales[:, g, cols]
+            if kind == "moving":
+                return mv_words[:, g, 4 * cols.start : 4 * cols.stop].bitcast(E4M3X4), mv_scales[:, g, cols]
+            return gate_codes[:, g, cols].bitcast(E4M3X4), gate_scales[:, g, cols]
+
+        def one_pass(acc, kind, m, g, cols):
+            codes, scales = weight(kind, g, cols)
+            nc.tensor.matmul_mx(
+                out=acc,
+                lhsT=phi_codes[:, m, g, :].bitcast(E4M3X4),
+                lhsT_scale=phi_scales[:, m, g, :],
+                rhs=codes,
+                rhs_scale=scales,
+                start=(g == 0),
+                stop=(g == PASSES - 1),
+            )
+
+        def passes(kind, m):
+            acc = bank_of(kind, m)
+            for g in range(PASSES):
+                one_pass(acc[:], kind, m, g, slice(0, N))
+
+        trusts = {}
+        terms = {}
+        logits = {}
+
+        def trust(m, func):
+            trusts[m] = stage.tile([P, N], F32, name=f"trust_{m}", tag="trust", bufs=3)
+            if func == ACT.Tanh:
+                nc.scalar.activation(trusts[m][:], bank_of("gate", m)[:], func, scale=0.5)
+            else:
+                nc.scalar.activation(trusts[m][:], bank_of("gate", m)[:], func)
+
+        def gated(m, func):
+            terms[m] = stage.tile([P, N], F32, name=f"term_{m}", tag="term", bufs=3)
+            if func == ACT.Tanh:
+                nc.vector.scalar_tensor_tensor(
+                    out=terms[m][:], in0=trusts[m][:], scalar=1.0, in1=bank_of("moving", m)[:], op0=ALU.add, op1=ALU.mult
+                )
+            else:
+                nc.vector.tensor_tensor(out=terms[m][:], in0=trusts[m][:], in1=bank_of("moving", m)[:], op=ALU.mult)
+
+        def logit(m, func, bank, cols):
+            if m not in logits:
+                logits[m] = keep.tile([P, N], F32, name=f"logit_{m}")
+            if func == ACT.Tanh:
+                nc.vector.scalar_tensor_tensor(
+                    out=logits[m][:, cols], in0=terms[m][:, cols], scalar=0.5, in1=bank, op0=ALU.mult, op1=ALU.add
+                )
+            else:
+                nc.vector.tensor_tensor(out=logits[m][:, cols], in0=terms[m][:, cols], in1=bank, op=ALU.add)
+
+        results = {}
+
+        def occupancy(m, cols):
+            if m not in results:
+                results[m] = keep.tile([P, N], F32, name=f"result_{m}")
+            nc.scalar.activation(results[m][:, cols], logits[m][:, cols], ACT.Sigmoid)
+
+        def store(m, cols):
+            nc.sync.dma_start(out=out[m * P : (m + 1) * P, cols], in_=results[m][:, cols])
+
+        ALL = slice(0, N)
+
+        on_scalar, on_vector = nc.scalar.copy, nc.vector.tensor_copy
+        LOW, HIGH = slice(0, N // 2), slice(N // 2, N)
+
+        def both(kind, g):
+            for m in range(2):
+                one_pass(bank_of(kind, m)[:], kind, m, g, ALL)
+
+        turn(0, 0)
+        turn(0, 1)
+        exps(0, 0)
+        exps(0, 1)
+        turn(1, 0)
+        turn(1, 1)
+        amplify(0, 0, 0, 1)
+        amplify(0, 0, 1, 1)
+        quantize(0, 0, 0, 1)
+        amplify(0, 1, 0, 1)
+        quantize(0, 0, 1, 1)
+        amplify(0, 1, 1, 1)
+        quantize(0, 1, 0, 1)
+        exps(1, 0)
+        amplify(1, 0, 0, 2)
+        quantize(0, 1, 1, 1)
+        passes("static", 0)
+        exps(1, 1)
+        amplify(1, 1, 0, 2)
+        quantize(1, 0, 0, 2)
+        gather_gate(0, on_scalar)
+        gather_gate(1, on_vector)
+        quantize(1, 1, 0, 2)
+        passes("static", 1)
+        turn(2, 0)
+        turn(2, 1)
+        both("moving", 0)
+        both("moving", 1)
+        gather_gate(2, on_vector, LOW)
+        gather_gate(2, on_scalar, HIGH)
+        quantize_gate(1)
+        quantize_gate(0)
+        both("gate", 0)
+        both("gate", 1)
+        both("moving", 2)
+        both("moving", 3)
+        exps(2, 0)
+        gather_gate(3, on_scalar, HIGH)
+        gather_gate(3, on_vector, LOW)
+        quantize_gate(2)
+        exps(2, 1)
+        quantize_gate(3)
+        turn(3, 0)
+        turn(3, 1)
+        both("gate", 2)
+        both("gate", 3)
+        amplify(2, 0, 0, 2)
+        amplify(2, 1, 0, 2)
+        quantize(2, 0, 0, 2)
+        exps(3, 0)
+        trust(0, ACT.Tanh)
+        quantize(2, 1, 0, 2)
+        trust(1, ACT.Tanh)
+        gated(0, ACT.Tanh)
+        exps(3, 1)
+        logit(0, ACT.Tanh, bank_of("static", 0)[:], ALL)
+        gated(1, ACT.Tanh)
+
+        for m in range(2, TILES):
+            func = ACT.Tanh if m <= LAST_EXP_STEP else ACT.Sigmoid
+            before = ACT.Tanh if m - 1 <= LAST_EXP_STEP else ACT.Sigmoid
+            ahead = m + 2 < TILES
+            if ahead:
+                turn(m + 2, 0)
+                turn(m + 2, 1)
+            passes("gate", m)
+            passes("moving", m)
+            logit(m - 1, before, bank_of("static", m - 1)[:], ALL)
+            if ahead:
+                exps(m + 2, 0)
+                exps(m + 2, 1)
+            else:
+                if m == LAST_EXP_STEP + 1:
+                    for done in range(m):
+                        if done == 2:
+                            trust(m, func)
+                        occupancy(done, ALL)
+                        store(done, ALL)
+                else:
+                    trust(m, func)
+                    occupancy(m - 1, ALL)
+                    store(m - 1, ALL)
+            if m + 1 < TILES:
+                amplify(m + 1, 0, 0, 2)
+                amplify(m + 1, 1, 0, 2)
+                quantize(m + 1, 0, 0, 2)
+                quantize(m + 1, 1, 0, 2)
+            if ahead:
+                trust(m, func)
+            gated(m, func)
+            if m < TILES - 1:
+                passes("static", m)
+            else:
+                for i, tag in enumerate(["static1", "turn0", "turn1", "gate0"]):
+                    cols = slice(P * i, P * (i + 1))
+                    acc = psum.tile([P, P], F32, name=f"last_{i}", tag=tag)
+                    for g in range(PASSES):
+                        one_pass(acc[:], "static", m, g, cols)
+                    logit(m, func, acc[:], cols)
+                    occupancy(m, cols)
+                    if i % 2 == 1:
+                        store(m, slice(P * (i - 1), P * (i + 1)))

@@ -87,14 +87,14 @@ def tile_hilbert_occupancy_map_s10_kernel(
         load_scales(st_scales, static_scales)
         load_x(1, 1)
         nc.sync.dma_start(out=st_words[:], in_=static_words.rearrange("g p b -> p g b"))
-        load_gate(0)
-        load_gate(1)
-        load_gate(2)
-        load_x(2, 1)
         load_scales(mv_scales, moving_scales)
         load_moving(0, 2)
-        load_gate(3)
+        load_gate(0)
+        load_gate(1)
         load_moving(2, 2)
+        load_gate(2)
+        load_x(2, 1)
+        load_gate(3)
         for m in range(3, TILES):
             load_x(m, 1)
 
@@ -144,10 +144,12 @@ def tile_hilbert_occupancy_map_s10_kernel(
                 in_=phi_tiles[m, h][:, i0 : i0 + n, :, :].rearrange("p g r t -> p (g r t)"),
             )
 
-        def gather_gate(g, copy, cols=slice(0, N)):
-            if g not in gate_tiles:
-                gate_tiles[g] = stage.tile([P, N, PACK], BF16, name=f"gate_{g}", tag="gate", bufs=4, align_bytes=64)
-            copy(out=gate_tiles[g][:, cols, :], in_=raw[g][:, :, cols].rearrange("p j n -> p n j"))
+        def gather_gate(g, copy):
+            gate_tiles[g] = stage.tile([P, N, PACK], BF16, name=f"gate_{g}", tag="gate", bufs=4, align_bytes=64)
+            copy(
+                out=gate_tiles[g][:].rearrange("p (c i) j -> p c j i", i=4),
+                in_=raw[g][:].rearrange("p j (c i) -> p c j i", i=4),
+            )
 
         def quantize_gate(g):
             nc.vector.quantize_mx(
@@ -230,11 +232,11 @@ def tile_hilbert_occupancy_map_s10_kernel(
         ALL = slice(0, N)
 
         on_scalar, on_vector = nc.scalar.copy, nc.vector.tensor_copy
-        LOW, HIGH = slice(0, N // 2), slice(N // 2, N)
 
-        def both(kind, g):
-            for m in range(2):
-                one_pass(bank_of(kind, m)[:], kind, m, g, ALL)
+        def some(kind, tiles, groups):
+            for g in groups:
+                for m in tiles:
+                    one_pass(bank_of(kind, m)[:], kind, m, g, ALL)
 
         turn(0, 0)
         turn(0, 1)
@@ -252,62 +254,66 @@ def tile_hilbert_occupancy_map_s10_kernel(
         exps(1, 0)
         amplify(1, 0, 0, 2)
         quantize(0, 1, 1, 1)
-        passes("static", 0)
+        some("static", [0], [0, 1])
+        some("moving", [0], [0, 1])
+        some("static", [0], [2, 3])
         exps(1, 1)
         amplify(1, 1, 0, 2)
         quantize(1, 0, 0, 2)
+        some("static", [1], [0, 1])
+        some("moving", [1], [0, 1])
         gather_gate(0, on_scalar)
         gather_gate(1, on_vector)
         quantize(1, 1, 0, 2)
-        passes("static", 1)
-        turn(2, 0)
-        turn(2, 1)
-        both("moving", 0)
-        both("moving", 1)
-        gather_gate(2, on_vector, LOW)
-        gather_gate(2, on_scalar, HIGH)
+        some("static", [1], [2, 3])
+        some("moving", [0, 1], [2, 3])
+        gather_gate(2, on_scalar)
         quantize_gate(1)
         quantize_gate(0)
-        both("gate", 0)
-        both("gate", 1)
-        both("moving", 2)
-        both("moving", 3)
+        turn(2, 0)
+        turn(2, 1)
+        some("gate", [0, 1], [0, 1])
         exps(2, 0)
-        gather_gate(3, on_scalar, HIGH)
-        gather_gate(3, on_vector, LOW)
-        quantize_gate(2)
         exps(2, 1)
-        quantize_gate(3)
-        turn(3, 0)
-        turn(3, 1)
-        both("gate", 2)
-        both("gate", 3)
+        gather_gate(3, on_vector)
+        quantize_gate(2)
         amplify(2, 0, 0, 2)
-        amplify(2, 1, 0, 2)
-        quantize(2, 0, 0, 2)
+        some("gate", [0, 1], [2])
+        turn(3, 0)
+        quantize_gate(3)
+        turn(3, 1)
+        some("gate", [0, 1], [3])
         exps(3, 0)
         trust(0, ACT.Tanh)
-        quantize(2, 1, 0, 2)
         trust(1, ACT.Tanh)
+        amplify(2, 1, 0, 2)
+        quantize(2, 0, 0, 2)
         gated(0, ACT.Tanh)
+        quantize(2, 1, 0, 2)
         exps(3, 1)
+        turn(4, 0)
         logit(0, ACT.Tanh, bank_of("static", 0)[:], ALL)
         gated(1, ACT.Tanh)
-
         for m in range(2, TILES):
             func = ACT.Tanh if m <= LAST_EXP_STEP else ACT.Sigmoid
             before = ACT.Tanh if m - 1 <= LAST_EXP_STEP else ACT.Sigmoid
             ahead = m + 2 < TILES
-            if ahead:
-                turn(m + 2, 0)
-                turn(m + 2, 1)
             passes("gate", m)
-            passes("moving", m)
-            logit(m - 1, before, bank_of("static", m - 1)[:], ALL)
+            if m == 2:
+                turn(4, 1)
             if ahead:
                 exps(m + 2, 0)
+                trust(m, func)
                 exps(m + 2, 1)
-            else:
+            passes("moving", m)
+            if m + 1 < TILES:
+                amplify(m + 1, 0, 0, 2)
+            logit(m - 1, before, bank_of("static", m - 1)[:], ALL)
+            if m + 1 < TILES:
+                amplify(m + 1, 1, 0, 2)
+                quantize(m + 1, 0, 0, 2)
+                quantize(m + 1, 1, 0, 2)
+            if not ahead:
                 if m == LAST_EXP_STEP + 1:
                     for done in range(m):
                         if done == 2:
@@ -318,16 +324,12 @@ def tile_hilbert_occupancy_map_s10_kernel(
                     trust(m, func)
                     occupancy(m - 1, ALL)
                     store(m - 1, ALL)
-            if m + 1 < TILES:
-                amplify(m + 1, 0, 0, 2)
-                amplify(m + 1, 1, 0, 2)
-                quantize(m + 1, 0, 0, 2)
-                quantize(m + 1, 1, 0, 2)
-            if ahead:
-                trust(m, func)
             gated(m, func)
             if m < TILES - 1:
                 passes("static", m)
+                if m + 3 < TILES:
+                    turn(m + 3, 0)
+                    turn(m + 3, 1)
             else:
                 for i, tag in enumerate(["static1", "turn0", "turn1", "gate0"]):
                     cols = slice(P * i, P * (i + 1))

@@ -91,11 +91,12 @@ def tile_hilbert_occupancy_map_s10_kernel(
         load_moving(0, 2)
         load_gate(0)
         load_gate(1)
-        load_moving(2, 2)
         load_gate(2)
         load_x(2, 1)
         load_gate(3)
-        for m in range(3, TILES):
+        load_x(3, 1)
+        load_moving(2, 2)
+        for m in range(4, TILES):
             load_x(m, 1)
 
         phi_codes = keep.tile([P, TILES, PASSES, P], U32, name="phi_codes", align_bytes=64)
@@ -115,15 +116,17 @@ def tile_hilbert_occupancy_map_s10_kernel(
             for i in range(HALF):
                 first = (HALF * h + i) * (K_PASS // 2)
                 for u in range(2):
-                    nc.tensor.transpose(bank[:, 2 * i + u, :], words[:, first + u : first + K_PASS // 2 : 2], identity[:])
+                    nc.tensor.transpose(bank[:, HALF * u + i, :], words[:, first + u : first + K_PASS // 2 : 2], identity[:])
 
-        def exps(m, h):
+        def exps(m, h, parts=1):
             tile = stage.tile([P, HALF, P, PACK], F32, name=f"exp_{m}_{h}", tag="exp", bufs=12)
             exp_tiles[m, h] = tile
-            bank = turned[m, h][:].rearrange("p b r -> p (b r)").bitcast(BF16)
-            for i in range(HALF):
-                src = bank[:, 512 * i : 512 * (i + 1)].rearrange("p (u r e) -> p r u e", u=2, e=2)
-                nc.scalar.activation(tile[:, i, :, :].rearrange("p r (u e) -> p r u e", u=2), src, ACT.Exp)
+            src = turned[m, h][:].rearrange("p b r -> p (b r)").bitcast(BF16).rearrange("p (u c e) -> p c u e", u=2, e=2)
+            dst = tile[:].rearrange("p i r t -> p (i r) t").rearrange("p c (u e) -> p c u e", u=2)
+            width = HALF * P // parts
+            for i in range(parts):
+                cols = slice(width * i, width * (i + 1))
+                nc.scalar.activation(dst[:, cols], src[:, cols], ACT.Exp)
 
         def amplify(m, h, i0, n):
             if (m, h) not in phi_tiles:
@@ -240,8 +243,8 @@ def tile_hilbert_occupancy_map_s10_kernel(
 
         turn(0, 0)
         turn(0, 1)
-        exps(0, 0)
-        exps(0, 1)
+        exps(0, 0, 2)
+        exps(0, 1, 2)
         turn(1, 0)
         turn(1, 1)
         amplify(0, 0, 0, 1)
@@ -266,33 +269,34 @@ def tile_hilbert_occupancy_map_s10_kernel(
         gather_gate(1, on_vector)
         quantize(1, 1, 0, 2)
         some("static", [1], [2, 3])
-        some("moving", [0, 1], [2, 3])
+        turn(2, 0)
+        turn(2, 1)
         gather_gate(2, on_scalar)
         quantize_gate(1)
         quantize_gate(0)
-        turn(2, 0)
-        turn(2, 1)
+        gather_gate(3, on_vector)
         some("gate", [0, 1], [0, 1])
         exps(2, 0)
-        exps(2, 1)
-        gather_gate(3, on_vector)
         quantize_gate(2)
-        amplify(2, 0, 0, 2)
-        some("gate", [0, 1], [2])
         turn(3, 0)
+        some("gate", [0, 1], [2])
         quantize_gate(3)
-        turn(3, 1)
+        exps(2, 1)
         some("gate", [0, 1], [3])
+        some("moving", [0, 1], [2, 3])
+        turn(3, 1)
+        amplify(2, 0, 0, 2)
         exps(3, 0)
         trust(0, ACT.Tanh)
-        trust(1, ACT.Tanh)
         amplify(2, 1, 0, 2)
         quantize(2, 0, 0, 2)
-        gated(0, ACT.Tanh)
+        trust(1, ACT.Tanh)
         quantize(2, 1, 0, 2)
+        gated(0, ACT.Tanh)
         exps(3, 1)
         turn(4, 0)
         logit(0, ACT.Tanh, bank_of("static", 0)[:], ALL)
+        amplify(3, 0, 0, 2)
         gated(1, ACT.Tanh)
         for m in range(2, TILES):
             func = ACT.Tanh if m <= LAST_EXP_STEP else ACT.Sigmoid
@@ -306,7 +310,7 @@ def tile_hilbert_occupancy_map_s10_kernel(
                 trust(m, func)
                 exps(m + 2, 1)
             passes("moving", m)
-            if m + 1 < TILES:
+            if m + 1 < TILES and m > 2:
                 amplify(m + 1, 0, 0, 2)
             logit(m - 1, before, bank_of("static", m - 1)[:], ALL)
             if m + 1 < TILES:

from contextlib import ExitStack

import concourse.mybir as mybir
from concourse.masks import make_identity

ROWS, K, N = 1024, 2048, 512
FLOPS = 3 * 2 * ROWS * K * N

F32 = mybir.dt.float32
BF16 = mybir.dt.bfloat16
U32 = mybir.dt.uint32
I32 = mybir.dt.int32
U8 = mybir.dt.uint8
E4M3X4 = mybir.dt.float8_e4m3fn_x4
E2M1X4 = mybir.dt.float4_e2m1fn_x4
ACT = mybir.ActivationFunctionType
ALU = mybir.AluOpType

P = 128
PACK = 4
K_PASS = P * PACK
PASSES = K // K_PASS
TILES = ROWS // P
HALF = PASSES // 2
LAST_EXP_STEP = TILES - 3


def tile_hilbert_occupancy_map_s10_kernel(
    tc, log_kernel, amplitude, static_words, static_scales, moving_words, moving_scales, w_gate, out
):
    nc = tc.nc
    with ExitStack() as ctx:
        keep = ctx.enter_context(tc.tile_pool(name="keep", bufs=1))
        stage = ctx.enter_context(tc.tile_pool(name="stage", bufs=4))
        psum = ctx.enter_context(tc.psum_pool(name="psum", bufs=1))
        ctx.enter_context(tc.manual_schedule())

        identity = keep.tile([P, P], F32, name="identity")
        make_identity(nc, identity[:])
        st_scales = keep.tile([P, PASSES, N], U8, name="st_scales", align_bytes=64)
        mv_scales = keep.tile([P, PASSES, N], U8, name="mv_scales", align_bytes=64)
        warm = keep.tile([P, 1], F32, name="warm")
        nc.vector.memset(warm[:], 0.0)
        nc.vector.memset(st_scales[:].rearrange("p g n -> p (g n)").bitcast(I32), 0)
        nc.vector.memset(mv_scales[:].rearrange("p g n -> p (g n)").bitcast(I32), 0)
        warm_out = keep.tile([P, 1], F32, name="warm_out")

        amp = keep.tile([P, PASSES, 1, PACK], BF16, name="amp")
        nc.scalar.dma_start(out=amp[:, :, 0, :], in_=amplitude.rearrange("(g p t) -> p g t", g=PASSES, t=PACK))

        nc.scalar.activation(warm_out[:], warm[:], ACT.Exp)

        x_tiles = []
        for m in range(TILES):
            x_tiles.append(keep.tile([P, K], BF16, name=f"x{m}", align_bytes=64))

        def load_x(m, parts):
            width = K // parts
            for i in range(parts):
                cols = slice(i * width, (i + 1) * width)
                nc.sync.dma_start(out=x_tiles[m][:, cols], in_=log_kernel[m * P : (m + 1) * P, cols])

        def load_scales(plane, source):
            for q in range(4):
                nc.sync.dma_start(
                    out=plane[32 * q : 32 * q + 4, :, :].bitcast(I32),
                    in_=source[:, 4 * q : 4 * q + 4, :].rearrange("g r n -> r g n").bitcast(I32),
                )

        st_words = keep.tile([P, PASSES, 2 * N], U8, name="st_words", align_bytes=64)
        mv_words = keep.tile([P, PASSES, 4 * N], U8, name="mv_words", align_bytes=64)
        raw = []
        for g in range(PASSES):
            raw.append(keep.tile([P, PACK, N], BF16, name=f"raw{g}", align_bytes=64))

        def load_gate(g):
            nc.sync.dma_start(
                out=raw[g][:], in_=w_gate[g * K_PASS : (g + 1) * K_PASS, :].rearrange("(p j) n -> p j n", j=PACK)
            )

        def load_moving(g0, n):
            nc.sync.dma_start(
                out=mv_words[:, g0 : g0 + n, :], in_=moving_words[g0 : g0 + n].rearrange("g p n t -> p g (n t)")
            )

        load_x(0, 2)
        load_scales(st_scales, static_scales)
        load_x(1, 1)
        nc.sync.dma_start(out=st_words[:], in_=static_words.rearrange("g p b -> p g b"))
        load_scales(mv_scales, moving_scales)
        load_moving(0, 2)
        load_gate(0)
        load_gate(1)
        load_gate(2)
        load_x(2, 1)
        load_gate(3)
        load_x(3, 1)
        load_moving(2, 2)
        for m in range(4, TILES):
            load_x(m, 1)

        phi_codes = keep.tile([P, TILES, PASSES, P], U32, name="phi_codes", align_bytes=64)
        phi_scales = keep.tile([P, TILES, PASSES, P], U8, name="phi_scales", align_bytes=64)
        gate_codes = keep.tile([P, PASSES, N], U32, name="gate_codes", align_bytes=64)
        gate_scales = keep.tile([P, PASSES, N], U8, name="gate_scales", align_bytes=64)

        exp_tiles = {}
        phi_tiles = {}
        turned = {}
        gate_tiles = {}

        def turn(m, h):
            bank = psum.tile([P, 2 * HALF, P], F32, name=f"turn_{m}_{h}", tag=f"turn{h}")
            turned[m, h] = bank
            words = x_tiles[m][:].bitcast(F32)
            for i in range(HALF):
                first = (HALF * h + i) * (K_PASS // 2)
                for u in range(2):
                    nc.tensor.transpose(bank[:, HALF * u + i, :], words[:, first + u : first + K_PASS // 2 : 2], identity[:])

        def exps(m, h, parts=1):
            tile = stage.tile([P, HALF, P, PACK], F32, name=f"exp_{m}_{h}", tag="exp", bufs=12)
            exp_tiles[m, h] = tile
            src = turned[m, h][:].rearrange("p b r -> p (b r)").bitcast(BF16).rearrange("p (u c e) -> p c u e", u=2, e=2)
            dst = tile[:].rearrange("p i r t -> p (i r) t").rearrange("p c (u e) -> p c u e", u=2)
            width = HALF * P // parts
            for i in range(parts):
                cols = slice(width * i, width * (i + 1))
                nc.scalar.activation(dst[:, cols], src[:, cols], ACT.Exp)

        def amplify(m, h, i0, n):
            if (m, h) not in phi_tiles:
                phi_tiles[m, h] = stage.tile([P, HALF, P, PACK], BF16, name=f"phi_{m}_{h}", tag="phi", bufs=4, align_bytes=64)
            g = HALF * h + i0
            nc.vector.tensor_tensor(
                out=phi_tiles[m, h][:, i0 : i0 + n, :, :],
                in0=exp_tiles[m, h][:, i0 : i0 + n, :, :],
                in1=amp[:, g : g + n, :, :].to_broadcast([P, n, P, PACK]),
                op=ALU.mult,
            )

        def quantize(m, h, i0, n):
            g = HALF * h + i0
            nc.vector.quantize_mx(
                out=phi_codes[:, m, g : g + n, :].rearrange("p g r -> p (g r)").bitcast(E4M3X4),
                scales=phi_scales[:, m, g : g + n, :].rearrange("p g r -> p (g r)"),
                in_=phi_tiles[m, h][:, i0 : i0 + n, :, :].rearrange("p g r t -> p (g r t)"),
            )

        def gather_gate(g, copy):
            gate_tiles[g] = stage.tile([P, N, PACK], BF16, name=f"gate_{g}", tag="gate", bufs=4, align_bytes=64)
            copy(
                out=gate_tiles[g][:].rearrange("p (c i) j -> p c j i", i=4),
                in_=raw[g][:].rearrange("p j (c i) -> p c j i", i=4),
            )

        def quantize_gate(g):
            nc.vector.quantize_mx(
                out=gate_codes[:, g, :].bitcast(E4M3X4),
                scales=gate_scales[:, g, :],
                in_=gate_tiles[g][:].rearrange("p n t -> p (n t)"),
            )

        banks = {}

        def bank_of(kind, m):
            if (kind, m) not in banks:
                banks[kind, m] = psum.tile([P, N], F32, name=f"{kind}_{m}", tag=f"{kind}{m % 2}")
            return banks[kind, m]

        def weight(kind, g, cols):
            if kind == "static":
                return st_words[:, g, 2 * cols.start : 2 * cols.stop].bitcast(E2M1X4), st_scales[:, g, cols]
            if kind == "moving":
                return mv_words[:, g, 4 * cols.start : 4 * cols.stop].bitcast(E4M3X4), mv_scales[:, g, cols]
            return gate_codes[:, g, cols].bitcast(E4M3X4), gate_scales[:, g, cols]

        def one_pass(acc, kind, m, g, cols):
            codes, scales = weight(kind, g, cols)
            nc.tensor.matmul_mx(
                out=acc,
                lhsT=phi_codes[:, m, g, :].bitcast(E4M3X4),
                lhsT_scale=phi_scales[:, m, g, :],
                rhs=codes,
                rhs_scale=scales,
                start=(g == 0),
                stop=(g == PASSES - 1),
            )

        def passes(kind, m):
            acc = bank_of(kind, m)
            for g in range(PASSES):
                one_pass(acc[:], kind, m, g, slice(0, N))

        trusts = {}
        terms = {}
        logits = {}

        def trust(m, func):
            trusts[m] = stage.tile([P, N], F32, name=f"trust_{m}", tag="trust", bufs=3)
            if func == ACT.Tanh:
                nc.scalar.activation(trusts[m][:], bank_of("gate", m)[:], func, scale=0.5)
            else:
                nc.scalar.activation(trusts[m][:], bank_of("gate", m)[:], func)

        def gated(m, func):
            terms[m] = stage.tile([P, N], F32, name=f"term_{m}", tag="term", bufs=3)
            if func == ACT.Tanh:
                nc.vector.scalar_tensor_tensor(
                    out=terms[m][:], in0=trusts[m][:], scalar=1.0, in1=bank_of("moving", m)[:], op0=ALU.add, op1=ALU.mult
                )
            else:
                nc.vector.tensor_tensor(out=terms[m][:], in0=trusts[m][:], in1=bank_of("moving", m)[:], op=ALU.mult)

        def logit(m, func, bank, cols):
            if m not in logits:
                logits[m] = keep.tile([P, N], F32, name=f"logit_{m}")
            if func == ACT.Tanh:
                nc.vector.scalar_tensor_tensor(
                    out=logits[m][:, cols], in0=terms[m][:, cols], scalar=0.5, in1=bank, op0=ALU.mult, op1=ALU.add
                )
            else:
                nc.vector.tensor_tensor(out=logits[m][:, cols], in0=terms[m][:, cols], in1=bank, op=ALU.add)

        results = {}

        def occupancy(m, cols):
            if m not in results:
                results[m] = keep.tile([P, N], F32, name=f"result_{m}")
            nc.scalar.activation(results[m][:, cols], logits[m][:, cols], ACT.Sigmoid)

        def store(m, cols):
            nc.sync.dma_start(out=out[m * P : (m + 1) * P, cols], in_=results[m][:, cols])

        ALL = slice(0, N)

        on_scalar, on_vector = nc.scalar.copy, nc.vector.tensor_copy

        def some(kind, tiles, groups):
            for g in groups:
                for m in tiles:
                    one_pass(bank_of(kind, m)[:], kind, m, g, ALL)

        turn(0, 0)
        turn(0, 1)
        exps(0, 0, 2)
        exps(0, 1, 2)
        turn(1, 0)
        turn(1, 1)
        amplify(0, 0, 0, 1)
        amplify(0, 0, 1, 1)
        quantize(0, 0, 0, 1)
        amplify(0, 1, 0, 1)
        quantize(0, 0, 1, 1)
        amplify(0, 1, 1, 1)
        quantize(0, 1, 0, 1)
        exps(1, 0)
        amplify(1, 0, 0, 2)
        quantize(0, 1, 1, 1)
        some("static", [0], [0, 1])
        some("moving", [0], [0, 1])
        some("static", [0], [2, 3])
        exps(1, 1)
        amplify(1, 1, 0, 2)
        quantize(1, 0, 0, 2)
        some("static", [1], [0, 1])
        some("moving", [1], [0, 1])
        gather_gate(0, on_scalar)
        gather_gate(1, on_vector)
        quantize(1, 1, 0, 2)
        some("static", [1], [2, 3])
        turn(2, 0)
        turn(2, 1)
        gather_gate(2, on_scalar)
        quantize_gate(1)
        quantize_gate(0)
        gather_gate(3, on_vector)
        some("gate", [0, 1], [0, 1])
        exps(2, 0)
        quantize_gate(2)
        turn(3, 0)
        some("gate", [0, 1], [2])
        quantize_gate(3)
        exps(2, 1)
        some("gate", [0, 1], [3])
        some("moving", [0, 1], [2, 3])
        turn(3, 1)
        amplify(2, 0, 0, 2)
        exps(3, 0)
        trust(0, ACT.Tanh)
        amplify(2, 1, 0, 2)
        quantize(2, 0, 0, 2)
        trust(1, ACT.Tanh)
        quantize(2, 1, 0, 2)
        gated(0, ACT.Tanh)
        exps(3, 1)
        turn(4, 0)
        logit(0, ACT.Tanh, bank_of("static", 0)[:], ALL)
        amplify(3, 0, 0, 2)
        gated(1, ACT.Tanh)
        for m in range(2, TILES):
            func = ACT.Tanh if m <= LAST_EXP_STEP else ACT.Sigmoid
            before = ACT.Tanh if m - 1 <= LAST_EXP_STEP else ACT.Sigmoid
            ahead = m + 2 < TILES
            passes("gate", m)
            if m == 2:
                turn(4, 1)
            if ahead:
                exps(m + 2, 0)
                trust(m, func)
                exps(m + 2, 1)
            passes("moving", m)
            if m + 1 < TILES and m > 2:
                amplify(m + 1, 0, 0, 2)
            logit(m - 1, before, bank_of("static", m - 1)[:], ALL)
            if m + 1 < TILES:
                amplify(m + 1, 1, 0, 2)
                quantize(m + 1, 0, 0, 2)
                quantize(m + 1, 1, 0, 2)
            if not ahead:
                if m == LAST_EXP_STEP + 1:
                    for done in range(m):
                        if done == 2:
                            trust(m, func)
                        occupancy(done, ALL)
                        store(done, ALL)
                else:
                    trust(m, func)
                    occupancy(m - 1, ALL)
                    store(m - 1, ALL)
            gated(m, func)
            if m < TILES - 1:
                passes("static", m)
                if m + 3 < TILES:
                    turn(m + 3, 0)
                    turn(m + 3, 1)
            else:
                for i, tag in enumerate(["static1", "turn0", "turn1", "gate0"]):
                    cols = slice(P * i, P * (i + 1))
                    acc = psum.tile([P, P], F32, name=f"last_{i}", tag=tag)
                    for g in range(PASSES):
                        one_pass(acc[:], "static", m, g, cols)
                    logit(m, func, acc[:], cols)
                    occupancy(m, cols)
                    if i % 2 == 1:
                        store(m, slice(P * (i - 1), P * (i + 1)))
